import numpy as np
import ml_dtypes


def mxq(x, axis, fmt="e4m3"):
    dtype, down = {"e4m3": (ml_dtypes.float8_e4m3fn, 7), "e5m2": (ml_dtypes.float8_e5m2, 14)}[fmt]
    v = np.moveaxis(np.asarray(x, np.float32).astype(ml_dtypes.bfloat16).astype(np.float64), axis, -1)
    blocks = v.reshape(v.shape[:-1] + (-1, 32))
    amax = np.abs(blocks).max(-1, keepdims=True)
    byte = np.maximum(np.where(amax > 0, np.frexp(amax)[1] - 1 + 127, 0) - down, 1)
    scale = np.exp2(byte - 127.0)
    codes = (blocks / scale).astype(np.float32).astype(dtype).astype(np.float64)
    return np.moveaxis((codes * scale).reshape(v.shape), -1, axis)


WIDE = False


def mx_kscale(k):
    if not WIDE:
        return np.ones(k)
    levels = np.array([10, -10, 5, -5, 0])
    if k % 512:
        return np.exp2(np.random.permutation(np.resize(levels, k // 32))).repeat(32)
    a = np.empty((k // 512, 16))
    for p in range(k // 512):
        a[p, :8] = np.random.permutation(np.resize(levels, 8))
        for g in range(8):
            far = levels[np.abs(levels - a[p, g]) >= 10]
            a[p, g + 8] = far[np.random.randint(len(far))]
    return np.exp2(a.ravel()).repeat(32)


BF16 = ml_dtypes.bfloat16


def bf(x):
    return np.asarray(x, np.float32).astype(BF16)


def f64(x):
    return np.asarray(x).astype(np.float64)

def planes(Y):
    n, m = Y.shape
    b = f64(bf(Y)).reshape(n // 32, 32, m)
    amax = np.abs(b).max(1)
    byte = np.clip(np.where(amax > 0, np.frexp(amax)[1] - 1 + 127 - 7, 1), 1, 254)
    codes = (b * np.exp2(127.0 - byte)[:, None, :]).reshape(n, m).astype(np.float32).astype(ml_dtypes.float8_e4m3fn).view(np.uint8)
    words = codes.reshape(n // 512, 128, 4, m).transpose(0, 1, 3, 2)
    return np.ascontiguousarray(words), np.ascontiguousarray(byte.astype(np.uint8).reshape(n // 512, 16, m))


T, D, N = 1024, 1024, 1024


def setup_inputs():
    c = mx_kscale(T)
    kr = np.random.uniform(0.6, 1.4, (T, 1))
    return {
        "x": bf(np.random.standard_normal((T, D))),
        "beta": bf(np.random.uniform(0.2, 2.0, (T, D))),
        "k": bf(np.random.standard_normal((T, N)) * kr),
        "gk": bf(np.random.uniform(0.3, 1.7, N)),
        "s": bf(2.0 * np.random.standard_normal((D, N))),
        "ga": bf(np.random.uniform(0.5, 1.1, T) * c),
        "gb": bf(np.random.uniform(0.8, 1.7, T) / c),
    }


def implicit_step(beta, m, ga):
    return ga[:, None] * beta / (1.0 + beta * m[:, None])


def core(x, beta, k, gk, s, ga, gb):
    x, beta, k, gk, s, ga, gb = f64(x), f64(beta), f64(k), f64(gk), f64(s), f64(ga), f64(gb)
    n = k.shape[1]

    kk = k * gk[None, :]
    kk2 = kk * kk
    m = np.mean(kk2, axis=1)

    delta = implicit_step(beta, m, ga)

    p = mxq(delta.T, 1, "e4m3") @ mxq(gb[:, None] * (kk2 - 1.0), 0, "e4m3")

    r = np.sum(delta * gb[:, None], axis=0)

    w = mxq((delta * x).T, 1, "e4m3") @ mxq(gb[:, None] * kk, 0, "e4m3")

    return s * np.exp(-(p + r[:, None]) / n) + w / np.sqrt(n)


def reference(x, beta, k, gk, s, ga, gb):
    R_out = core(x, beta, k, gk, s, ga, gb)
    words, scales = planes(R_out)
    return R_out, words, scales

@@ -1,0 +1,362 @@
+from contextlib import ExitStack
+
+import concourse.mybir as mybir
+from concourse.masks import make_identity
+
+T, D, N = 1024, 1024, 1024
+FLOPS = 2 * 2 * T * D * N + 2 * T * D
+
+F32 = mybir.dt.float32
+BF16 = mybir.dt.bfloat16
+U32 = mybir.dt.uint32
+I32 = mybir.dt.int32
+U8 = mybir.dt.uint8
+FP8X4 = mybir.dt.float8_e4m3fn_x4
+ACT = mybir.ActivationFunctionType
+ALU = mybir.AluOpType
+AX = mybir.AxisListType
+
+P = 128
+PACK = 4
+GROUPS = 2
+HALF = 512
+B1_ON_VECTOR = ((0, 0),)
+B1_SCALE_ON_VECTOR = ((0, 0), (0, 1))
+
+
+def tile_chunkdecayedstateplusundecayedwrites_kernel(tc, x, beta, k, gk, s, ga, gb, out_0, out_1, out_2):
+    nc = tc.nc
+    with ExitStack() as ctx:
+        const = ctx.enter_context(tc.tile_pool(name="const", bufs=1))
+        rows = ctx.enter_context(tc.tile_pool(name="rows", bufs=8))
+        big = ctx.enter_context(tc.tile_pool(name="big", bufs=6))
+        mixed = ctx.enter_context(tc.tile_pool(name="mixed", bufs=6))
+        codes = ctx.enter_context(tc.tile_pool(name="codes", bufs=1))
+        planes = ctx.enter_context(tc.tile_pool(name="planes", bufs=2))
+        psum = ctx.enter_context(tc.psum_pool(name="psum", bufs=8))
+        ctx.enter_context(tc.manual_schedule())
+
+        gk_row = const.tile([P, N], BF16, name="gk_row")
+        ones = const.tile([P, P], BF16, name="ones")
+        warm = const.tile([P, 1], F32, name="warm")
+        gab = const.tile([P, 8], BF16, name="gab")
+        gbb = const.tile([P, 8], BF16, name="gbb")
+        gaf = const.tile([P, 8], F32, name="gaf")
+        gbf = const.tile([P, 8], F32, name="gbf")
+        gb_up = const.tile([P, 8], F32, name="gb_up")
+        gb_neg = const.tile([P, 8], F32, name="gb_neg")
+        gb_r = const.tile([P, 8], F32, name="gb_r")
+        msq = const.tile([P, 8], F32, name="msq")
+        nr = const.tile([P, 8], F32, name="nr")
+
+        ident = const.tile([P, P], F32, name="ident")
+        r_sb = const.tile([P, D], F32, name="r_sb")
+        nc.vector.memset(gk_row[:, 0:512], 0.0)
+        nc.gpsimd.memset(gk_row[:, 512:1024], 0.0)
+        nc.vector.memset(ones[:], 1.0)
+        make_identity(nc, ident[:])
+        nc.scalar.dma_start(out=gk_row[0:1, :], in_=gk.rearrange("(o n) -> o n", o=1))
+        nc.scalar.dma_start(out=gbb[:].rearrange("p (g j) -> p g j", g=2), in_=gb.rearrange("(g p j) -> p g j", g=2, j=PACK))
+        nc.scalar.dma_start(out=gab[:].rearrange("p (g j) -> p g j", g=2), in_=ga.rearrange("(g p j) -> p g j", g=2, j=PACK))
+        nc.scalar.activation(out=warm[:], in_=ones[:, 0:1], func=ACT.Abs_reciprocal_sqrt)
+
+        def load(name, src, g):
+            t = rows.tile([P, PACK, 1024], BF16, name=name, tag="row")
+            return t, src[g * 512 : (g + 1) * 512, :].rearrange("(p j) c -> p j c", j=PACK)
+
+        kt, bt, xt, st = [], [], [], []
+        for g in range(GROUPS):
+            t, view = load("k%d" % g, k, g)
+            step = 1 if g == 0 else 2
+            for j in range(0, PACK, step):
+                nc.sync.dma_start(out=t[:, j : j + step, :], in_=view[:, j : j + step, :])
+            kt.append(t)
+        for lst, src, name in ((bt, beta, "b"), (xt, x, "x"), (st, s, "s")):
+            for g in range(GROUPS):
+                t, view = load("%s%d" % (name, g), src, g)
+                nc.sync.dma_start(out=t[:], in_=view)
+                lst.append(t)
+
+        gk_ps = []
+        for h in range(2):
+            ps = psum.tile([P, HALF], F32, name="gk_ps%d" % h, tag="acc")
+            nc.tensor.matmul(out=ps[:], lhsT=ones[:], rhs=gk_row[:, h * HALF : (h + 1) * HALF], start=True, stop=True)
+            gk_ps.append(ps)
+
+        kk = [big.tile([P, PACK, N], F32, name="kk%d" % g, tag="big") for g in range(GROUPS)]
+        kk2 = [big.tile([P, PACK, N], F32, name="kks%d" % g, tag="big") for g in range(GROUPS)]
+        dl = [big.tile([P, PACK, D], F32, name="dl%d" % g, tag="big") for g in range(GROUPS)]
+        for g in range(GROUPS):
+            for j in range(PACK):
+                for h in range(2):
+                    hs = slice(h * HALF, (h + 1) * HALF)
+                    nc.vector.tensor_tensor(out=kk[g][:, j, hs], in0=kt[g][:, j, hs], in1=gk_ps[h][:], op=ALU.mult)
+                c = 4 * g + j
+                nc.scalar.activation(out=kk2[g][:, j, :], in_=kk[g][:, j, :], func=ACT.Square, scale=1.0 / 32.0, accum_out=msq[:, c : c + 1])
+            if g == 0:
+                nc.vector.tensor_copy(out=gbf[:], in_=gbb[:])
+                nc.vector.tensor_copy(out=gaf[:], in_=gab[:])
+                nc.vector.tensor_scalar(out=gb_up[:], in0=gbb[:], scalar1=1024.0, scalar2=None, op0=ALU.mult)
+                nc.vector.tensor_scalar(out=gb_neg[:], in0=gbb[:], scalar1=-1.0, scalar2=None, op0=ALU.mult)
+                nc.vector.tensor_scalar(out=gb_r[:], in0=gbb[:], scalar1=-1.0 / 1024.0, scalar2=None, op0=ALU.mult)
+
+        def operand(name):
+            c = [codes.tile([P, 1024], U32, name="%s_c%d" % (name, g), align_bytes=64) for g in range(GROUPS)]
+            z = [codes.tile([P, 1024], U8, name="%s_s%d" % (name, g), align_bytes=64) for g in range(GROUPS)]
+            return c, z
+
+        b1c, b1s = operand("b1")
+        b2c, b2s = operand("b2")
+        a1c, a1s = operand("a1")
+        a2c, a2s = operand("a2")
+
+        def mix():
+            return mixed.tile([P, HALF, PACK], BF16, name="mix", tag="mix", align_bytes=64)
+
+        def quant(op_c, op_s, g, h, m):
+            hs = slice(h * HALF, (h + 1) * HALF)
+            nc.vector.quantize_mx(out=op_c[g][:, hs].bitcast(FP8X4), scales=op_s[g][:, hs], in_=m[:].rearrange("p c j -> p (c j)"))
+
+        def outer(m):
+            return m.rearrange("p (c i) j -> p c j i", i=4)
+
+        def inner(t):
+            return t.rearrange("p j (c i) -> p c j i", i=4)
+
+        def b2_mix(g, h):
+            m = mix()
+            hs = slice(h * HALF, (h + 1) * HALF)
+            gbv = gbf[:, 4 * g : 4 * g + 4].unsqueeze(1).unsqueeze(3).to_broadcast([P, HALF // 4, PACK, 4])
+            nc.vector.tensor_tensor(out=outer(m[:]), in0=inner(kk[g][:, :, hs]), in1=gbv, op=ALU.mult)
+            return m
+
+        def rsq(g, j):
+            c = 4 * g + j
+            nc.scalar.activation(
+                out=dl[g][:, j, :].rearrange("p (G t m) -> p G t m", G=2, t=4),
+                in_=bt[g][:, j, :].rearrange("p (G m t) -> p G t m", G=2, t=4),
+                func=ACT.Abs_reciprocal_sqrt, scale=msq[:, c : c + 1], bias=1.0)
+
+        def sqh(g, G):
+            v = dl[g][:, :, G * HALF : (G + 1) * HALF]
+            nc.scalar.activation(out=v, in_=v, func=ACT.Square)
+
+        def delta(g, j, G):
+            c = 4 * g + j
+            v = dl[g][:, j, G * HALF : (G + 1) * HALF].rearrange("p (t m) -> p t m", t=4)
+            nc.vector.scalar_tensor_tensor(
+                out=v, in0=v, scalar=gaf[:, c : c + 1],
+                in1=bt[g][:, j, G * HALF : (G + 1) * HALF].rearrange("p (m t) -> p t m", t=4),
+                op0=ALU.mult, op1=ALU.mult)
+
+        def a1_mix(g, G):
+            m = mix()
+            nc.scalar.copy(out=outer(m[:]), in_=inner(dl[g][:, :, G * HALF : (G + 1) * HALF]))
+            return m
+
+        def a2_mix(g, G):
+            m = mix()
+            xv = xt[g][:, :, G * HALF : (G + 1) * HALF].rearrange("p j (m t) -> p t j m", t=4)
+            for t in range(4):
+                c0 = G * HALF + t * P
+                nc.vector.tensor_tensor(
+                    out=outer(m[:, t * P : (t + 1) * P, :]), in0=inner(dl[g][:, :, c0 : c0 + P]),
+                    in1=inner(xv[:, t]), op=ALU.mult)
+            return m
+
+        def b1_scale(g, j):
+            c = 4 * g + j
+            v = kk2[g][:, j, :]
+            if (g, j) in B1_SCALE_ON_VECTOR:
+                nc.vector.tensor_scalar(out=v, in0=v, scalar1=1.0 / 1024.0, scalar2=gb_up[:, c : c + 1], op0=ALU.subtract, op1=ALU.mult)
+            else:
+                nc.scalar.activation(out=v, in_=v, func=ACT.Identity, scale=gb_up[:, c : c + 1], bias=gb_neg[:, c : c + 1])
+
+        def b1_mix(g, h):
+            m = mix()
+            src = inner(kk2[g][:, :, h * HALF : (h + 1) * HALF])
+            if (g, h) in B1_ON_VECTOR:
+                nc.vector.tensor_copy(out=outer(m[:]), in_=src)
+            else:
+                nc.scalar.copy(out=outer(m[:]), in_=src)
+            return m
+
+        def r_part(r_ps, g, j, G):
+            c = 4 * g + j
+            nc.tensor.matmul(out=r_ps[:], lhsT=gb_r[:, c : c + 1].to_broadcast([P, P]), rhs=dl[g][:, j, G * HALF : (G + 1) * HALF], start=(c == 0), stop=(c == 7))
+
+        def r_out(r_ps, G):
+            nc.scalar.copy(out=r_sb[:, G * HALF : (G + 1) * HALF], in_=r_ps[:])
+
+        def r_turn(G):
+            tr = psum.tile([P, HALF], F32, name="tr", tag="acc")
+            for t in range(4):
+                c0 = G * HALF + t * P
+                nc.tensor.transpose(tr[:, t * P : (t + 1) * P], r_sb[:, c0 : c0 + P], ident[:])
+            return tr
+
+        def r_keep(tr, G):
+            nc.vector.tensor_copy(out=nr[:, 4 * G : 4 * G + 4], in_=tr[:].rearrange("p (t m) -> p t m", t=4)[:, :, 0])
+
+        for g in range(GROUPS):
+            for j in range(PACK):
+                rsq(g, j)
+        for G in range(2):
+            for g in range(GROUPS):
+                sqh(g, G)
+        m00 = b2_mix(0, 0)
+        m01 = b2_mix(0, 1)
+        quant(b2c, b2s, 0, 0, m00)
+        m10 = b2_mix(1, 0)
+        quant(b2c, b2s, 0, 1, m01)
+        m11 = b2_mix(1, 1)
+        quant(b2c, b2s, 1, 0, m10)
+        for g, j in B1_SCALE_ON_VECTOR:
+            b1_scale(g, j)
+        r_ps = [psum.tile([P, HALF], F32, name="r_ps%d" % G, tag="acc") for G in range(2)]
+        for G in range(2):
+            for g in range(GROUPS):
+                for j in range(PACK):
+                    delta(g, j, G)
+                    r_part(r_ps[G], g, j, G)
+                if G == 0 and g == 0:
+                    quant(b2c, b2s, 1, 1, m11)
+        for g in range(GROUPS):
+            for j in range(PACK):
+                if (g, j) not in B1_SCALE_ON_VECTOR:
+                    b1_scale(g, j)
+            if g == 0:
+                a1m = [a1_mix(0, 0)]
+        a2m = [a2_mix(0, 0)]
+        a2m.append(a2_mix(1, 0))
+        r_out(r_ps[0], 0)
+        a1m.append(a1_mix(1, 0))
+        r_out(r_ps[1], 1)
+        tr0 = r_turn(0)
+        tr1 = r_turn(1)
+        b1m = {}
+        b1m[0, 0] = b1_mix(0, 0)
+        quant(a2c, a2s, 0, 0, a2m[0])
+        quant(a1c, a1s, 0, 0, a1m[0])
+        b1m[1, 0] = b1_mix(1, 0)
+        quant(a2c, a2s, 1, 0, a2m[1])
+        quant(a1c, a1s, 1, 0, a1m[1])
+        r_keep(tr0, 0)
+        r_keep(tr1, 1)
+        b1m[0, 1] = b1_mix(0, 1)
+        quant(b1c, b1s, 0, 0, b1m[0, 0])
+        a2n = [a2_mix(0, 1)]
+        quant(b1c, b1s, 1, 0, b1m[1, 0])
+        b1m[1, 1] = b1_mix(1, 1)
+        quant(b1c, b1s, 0, 1, b1m[0, 1])
+        a2n.append(a2_mix(1, 1))
+        quant(b1c, b1s, 1, 1, b1m[1, 1])
+        quant(a2c, a2s, 0, 1, a2n[0])
+        quant(a2c, a2s, 1, 1, a2n[1])
+
+        accs, sums, scale_planes = {}, {}, {}
+
+        def product(u, ac, asc, bc, bsc, which):
+            G, h = u
+            hs = slice(h * HALF, (h + 1) * HALF)
+            for t in range(4):
+                ds = slice(G * HALF + t * P, G * HALF + (t + 1) * P)
+                acc = psum.tile([P, HALF], F32, name="acc_" + which, tag="acc")
+                for g in range(GROUPS):
+                    nc.tensor.matmul_mx(
+                        out=acc[:], lhsT=ac[g][:, ds].bitcast(FP8X4), lhsT_scale=asc[g][:, ds],
+                        rhs=bc[g][:, hs].bitcast(FP8X4), rhs_scale=bsc[g][:, hs],
+                        start=(g == 0), stop=(g == GROUPS - 1))
+                accs[u, which, t] = acc
+
+        def decay(u):
+            G, h = u
+            sums[u] = rows.tile([P, PACK, HALF], F32, name="e%d%d" % u, tag="row")
+            for t in range(4):
+                nc.scalar.activation(out=sums[u][:, t, :], in_=accs[u, "p", t][:], func=ACT.Exp, scale=-1.0 / N, bias=nr[:, 4 * G + t : 4 * G + t + 1])
+
+        def times_state(u):
+            G, h = u
+            for t in (0, 2):
+                v = sums[u][:, t : t + 2, :]
+                nc.vector.tensor_tensor(out=v, in0=v, in1=st[G][:, t : t + 2, h * HALF : (h + 1) * HALF], op=ALU.mult)
+
+        def add_write(u, lo=0, hi=HALF):
+            for t in range(4):
+                v = sums[u][:, t, lo:hi]
+                nc.vector.scalar_tensor_tensor(out=v, in0=accs[u, "w", t][:, lo:hi], scalar=1.0 / 32.0, in1=v, op0=ALU.mult, op1=ALU.add)
+
+        def store(u, lo=0, hi=HALF):
+            G, h = u
+            nc.sync.dma_start(
+                out=out_0[G * 512 : (G + 1) * 512, h * HALF + lo : h * HALF + hi].rearrange("(p t) n -> p t n", t=4), in_=sums[u][:, :, lo:hi])
+
+        def round_out(u, m, lo=0, hi=HALF, engine_copy=nc.scalar.copy):
+            engine_copy(out=outer(m[:, lo:hi, :]), in_=inner(sums[u][:, :, lo:hi]))
+            return m
+
+        words = {}
+
+        def plane_out(u, m, lo=0, hi=HALF):
+            G, h = u
+            if lo == 0:
+                words[u] = planes.tile([P, HALF], U32, name="w_out", tag="w", align_bytes=64)
+            if h == 0:
+                scale_planes[G] = planes.tile([P, N], U8, name="s_out", tag="s", align_bytes=64)
+            w, z = words[u], scale_planes[G]
+            cols = slice(h * HALF + lo, h * HALF + hi)
+            nc.vector.quantize_mx(out=w[:, lo:hi].bitcast(FP8X4), scales=z[:, cols], in_=m[:, lo:hi, :].rearrange("p c j -> p (c j)"))
+            nc.sync.dma_start(out=out_1[G][:, cols, :].rearrange("p n j -> p (n j)").bitcast(I32), in_=w[:, lo:hi].bitcast(I32))
+            if h == 1 and hi == HALF:
+                queue = nc.sync if G == 0 else nc.scalar
+                for q in range(4):
+                    queue.dma_start(out=out_2[G][4 * q : 4 * q + 4, :].bitcast(I32), in_=z[32 * q : 32 * q + 4, :].bitcast(I32))
+
+        units = [(0, 0), (0, 1), (1, 0), (1, 1)]
+        A1, B1, A2, B2 = (a1c, a1s), (b1c, b1s), (a2c, a2s), (b2c, b2s)
+        rounded = {}
+
+        def finish(i):
+            add_write(units[i])
+            store(units[i])
+
+        def products(i, which):
+            product(units[i], *((A1 + B1) if which == "p" else (A2 + B2)), which)
+
+        products(0, "w")
+        products(0, "p")
+        decay(units[0])
+        a1n = [a1_mix(0, 1)]
+        products(1, "p")
+        times_state(units[0])
+        decay(units[1])
+        a1n.append(a1_mix(1, 1))
+        finish(0)
+        products(1, "w")
+        rounded[0] = round_out(units[0], mix())
+        times_state(units[1])
+        finish(1)
+        quant(a1c, a1s, 0, 1, a1n[0])
+        quant(a1c, a1s, 1, 1, a1n[1])
+        products(2, "w")
+        products(2, "p")
+        rounded[1] = round_out(units[1], mix())
+        plane_out(units[0], rounded[0])
+        decay(units[2])
+        plane_out(units[1], rounded[1])
+        times_state(units[2])
+        products(3, "p")
+        decay(units[3])
+        finish(2)
+        products(3, "w")
+        rounded[2] = round_out(units[2], mix())
+        times_state(units[3])
+        plane_out(units[2], rounded[2])
+        last, m = units[3], mix()
+        for lo in (0, 256):
+            add_write(last, lo, lo + 256)
+            store(last, lo, lo + 256)
+        for lo, engine_copy in ((0, nc.scalar.copy), (256, nc.vector.tensor_copy)):
+            round_out(last, m, lo, lo + 256, engine_copy)
+        for lo in (0, 256):
+            plane_out(last, m, lo, lo + 256)

@@ -20,8 +20,7 @@ P = 128
 PACK = 4
 GROUPS = 2
 HALF = 512
-B1_ON_VECTOR = ((0, 0),)
-B1_SCALE_ON_VECTOR = ((0, 0), (0, 1))
+KK_ON_GPSIMD = ((0, 3), (1, 3))
 
 
 def tile_chunkdecayedstateplusundecayedwrites_kernel(tc, x, beta, k, gk, s, ga, gb, out_0, out_1, out_2):
@@ -41,21 +40,18 @@ def tile_chunkdecayedstateplusundecayedwrites_kernel(tc, x, beta, k, gk, s, ga, 
         warm = const.tile([P, 1], F32, name="warm")
         gab = const.tile([P, 8], BF16, name="gab")
         gbb = const.tile([P, 8], BF16, name="gbb")
-        gaf = const.tile([P, 8], F32, name="gaf")
-        gbf = const.tile([P, 8], F32, name="gbf")
         gb_up = const.tile([P, 8], F32, name="gb_up")
-        gb_neg = const.tile([P, 8], F32, name="gb_neg")
         gb_r = const.tile([P, 8], F32, name="gb_r")
         msq = const.tile([P, 8], F32, name="msq")
         nr = const.tile([P, 8], F32, name="nr")
 
         ident = const.tile([P, P], F32, name="ident")
-        r_sb = const.tile([P, D], F32, name="r_sb")
-        nc.vector.memset(gk_row[:, 0:512], 0.0)
-        nc.gpsimd.memset(gk_row[:, 512:1024], 0.0)
+        nc.vector.memset(gk_row[:], 0.0)
         nc.vector.memset(ones[:], 1.0)
         make_identity(nc, ident[:])
-        nc.scalar.dma_start(out=gk_row[0:1, :], in_=gk.rearrange("(o n) -> o n", o=1))
+        ident_b = const.tile([P, P], BF16, name="ident_b")
+        nc.gpsimd.tensor_copy(out=ident_b[:], in_=ident[:])
+        gk_sb = const.tile([P, N], BF16, name="gk_sb")
         nc.scalar.dma_start(out=gbb[:].rearrange("p (g j) -> p g j", g=2), in_=gb.rearrange("(g p j) -> p g j", g=2, j=PACK))
         nc.scalar.dma_start(out=gab[:].rearrange("p (g j) -> p g j", g=2), in_=ga.rearrange("(g p j) -> p g j", g=2, j=PACK))
         nc.scalar.activation(out=warm[:], in_=ones[:, 0:1], func=ACT.Abs_reciprocal_sqrt)
@@ -70,6 +66,8 @@ def tile_chunkdecayedstateplusundecayedwrites_kernel(tc, x, beta, k, gk, s, ga, 
             step = 1 if g == 0 else 2
             for j in range(0, PACK, step):
                 nc.sync.dma_start(out=t[:, j : j + step, :], in_=view[:, j : j + step, :])
+                if g == 0 and j == 0:
+                    nc.sync.dma_start(out=gk_row[0:1, :], in_=gk.rearrange("(o n) -> o n", o=1))
             kt.append(t)
         for lst, src, name in ((bt, beta, "b"), (xt, x, "x"), (st, s, "s")):
             for g in range(GROUPS):
@@ -82,23 +80,36 @@ def tile_chunkdecayedstateplusundecayedwrites_kernel(tc, x, beta, k, gk, s, ga, 
             ps = psum.tile([P, HALF], F32, name="gk_ps%d" % h, tag="acc")
             nc.tensor.matmul(out=ps[:], lhsT=ones[:], rhs=gk_row[:, h * HALF : (h + 1) * HALF], start=True, stop=True)
             gk_ps.append(ps)
+            nc.scalar.copy(out=gk_sb[:, h * HALF : (h + 1) * HALF], in_=ps[:])
+        gb_ps = psum.tile([P, HALF], F32, name="gb_ps", tag="acc")
+        nc.tensor.matmul(out=gb_ps[:, 0:8], lhsT=ident_b[:], rhs=gbb[:], start=True, stop=True)
 
         kk = [big.tile([P, PACK, N], F32, name="kk%d" % g, tag="big") for g in range(GROUPS)]
         kk2 = [big.tile([P, PACK, N], F32, name="kks%d" % g, tag="big") for g in range(GROUPS)]
         dl = [big.tile([P, PACK, D], F32, name="dl%d" % g, tag="big") for g in range(GROUPS)]
-        for g in range(GROUPS):
-            for j in range(PACK):
-                for h in range(2):
-                    hs = slice(h * HALF, (h + 1) * HALF)
-                    nc.vector.tensor_tensor(out=kk[g][:, j, hs], in0=kt[g][:, j, hs], in1=gk_ps[h][:], op=ALU.mult)
-                c = 4 * g + j
-                nc.scalar.activation(out=kk2[g][:, j, :], in_=kk[g][:, j, :], func=ACT.Square, scale=1.0 / 32.0, accum_out=msq[:, c : c + 1])
-            if g == 0:
-                nc.vector.tensor_copy(out=gbf[:], in_=gbb[:])
-                nc.vector.tensor_copy(out=gaf[:], in_=gab[:])
-                nc.vector.tensor_scalar(out=gb_up[:], in0=gbb[:], scalar1=1024.0, scalar2=None, op0=ALU.mult)
-                nc.vector.tensor_scalar(out=gb_neg[:], in0=gbb[:], scalar1=-1.0, scalar2=None, op0=ALU.mult)
-                nc.vector.tensor_scalar(out=gb_r[:], in0=gbb[:], scalar1=-1.0 / 1024.0, scalar2=None, op0=ALU.mult)
+        def scale_keys(g, j0, j1):
+            for h in range(2):
+                hs = slice(h * HALF, (h + 1) * HALF)
+                nc.vector.tensor_tensor(
+                    out=kk[g][:, j0:j1, hs], in0=kt[g][:, j0:j1, hs],
+                    in1=gk_ps[h][:].unsqueeze(1).to_broadcast([P, j1 - j0, HALF]), op=ALU.mult)
+
+        def square(g, j):
+            c = 4 * g + j
+            nc.scalar.activation(out=kk2[g][:, j, :], in_=kk[g][:, j, :], func=ACT.Square, scale=1.0 / 32.0, accum_out=msq[:, c : c + 1])
+
+        nc.gpsimd.tensor_scalar(out=gb_up[:], in0=gbb[:], scalar1=1024.0, scalar2=0.0, op0=ALU.mult, op1=ALU.add)
+        nc.gpsimd.tensor_scalar(out=gb_r[:], in0=gbb[:], scalar1=-1.0 / 1024.0, scalar2=0.0, op0=ALU.mult, op1=ALU.add)
+        for g, j in KK_ON_GPSIMD:
+            nc.gpsimd.tensor_tensor(out=kk[g][:, j, :], in0=kt[g][:, j, :], in1=gk_sb[:], op=ALU.mult)
+        for j in range(3):
+            scale_keys(0, j, j + 1)
+            square(0, j)
+        square(0, 3)
+        scale_keys(1, 0, 2)
+        scale_keys(1, 2, 3)
+        for j in range(PACK):
+            square(1, j)
 
         def operand(name):
             c = [codes.tile([P, 1024], U32, name="%s_c%d" % (name, g), align_bytes=64) for g in range(GROUPS)]
@@ -126,7 +137,7 @@ def tile_chunkdecayedstateplusundecayedwrites_kernel(tc, x, beta, k, gk, s, ga, 
         def b2_mix(g, h):
             m = mix()
             hs = slice(h * HALF, (h + 1) * HALF)
-            gbv = gbf[:, 4 * g : 4 * g + 4].unsqueeze(1).unsqueeze(3).to_broadcast([P, HALF // 4, PACK, 4])
+            gbv = gb_ps[:, 4 * g : 4 * g + 4].unsqueeze(1).unsqueeze(3).to_broadcast([P, HALF // 4, PACK, 4])
             nc.vector.tensor_tensor(out=outer(m[:]), in0=inner(kk[g][:, :, hs]), in1=gbv, op=ALU.mult)
             return m
 
@@ -145,7 +156,7 @@ def tile_chunkdecayedstateplusundecayedwrites_kernel(tc, x, beta, k, gk, s, ga, 
             c = 4 * g + j
             v = dl[g][:, j, G * HALF : (G + 1) * HALF].rearrange("p (t m) -> p t m", t=4)
             nc.vector.scalar_tensor_tensor(
-                out=v, in0=v, scalar=gaf[:, c : c + 1],
+                out=v, in0=v, scalar=gab[:, c : c + 1],
                 in1=bt[g][:, j, G * HALF : (G + 1) * HALF].rearrange("p (m t) -> p t m", t=4),
                 op0=ALU.mult, op1=ALU.mult)
 
@@ -167,32 +178,27 @@ def tile_chunkdecayedstateplusundecayedwrites_kernel(tc, x, beta, k, gk, s, ga, 
         def b1_scale(g, j):
             c = 4 * g + j
             v = kk2[g][:, j, :]
-            if (g, j) in B1_SCALE_ON_VECTOR:
-                nc.vector.tensor_scalar(out=v, in0=v, scalar1=1.0 / 1024.0, scalar2=gb_up[:, c : c + 1], op0=ALU.subtract, op1=ALU.mult)
-            else:
-                nc.scalar.activation(out=v, in_=v, func=ACT.Identity, scale=gb_up[:, c : c + 1], bias=gb_neg[:, c : c + 1])
+            nc.gpsimd.tensor_scalar(out=v, in0=v, scalar1=-1.0 / 1024.0, scalar2=gb_up[:, c : c + 1], op0=ALU.add, op1=ALU.mult)
 
-        def b1_mix(g, h):
+        def b1_mix(g, h, engine_copy=nc.scalar.copy):
             m = mix()
             src = inner(kk2[g][:, :, h * HALF : (h + 1) * HALF])
-            if (g, h) in B1_ON_VECTOR:
-                nc.vector.tensor_copy(out=outer(m[:]), in_=src)
-            else:
-                nc.scalar.copy(out=outer(m[:]), in_=src)
+            engine_copy(out=outer(m[:]), in_=src)
             return m
 
         def r_part(r_ps, g, j, G):
             c = 4 * g + j
             nc.tensor.matmul(out=r_ps[:], lhsT=gb_r[:, c : c + 1].to_broadcast([P, P]), rhs=dl[g][:, j, G * HALF : (G + 1) * HALF], start=(c == 0), stop=(c == 7))
 
-        def r_out(r_ps, G):
-            nc.scalar.copy(out=r_sb[:, G * HALF : (G + 1) * HALF], in_=r_ps[:])
+        def r_out(r_ps):
+            r_sb = planes.tile([P, HALF], F32, name="r_sb", tag="w", align_bytes=64)
+            nc.scalar.copy(out=r_sb[:], in_=r_ps[:])
+            return r_sb
 
-        def r_turn(G):
+        def r_turn(r_sb):
             tr = psum.tile([P, HALF], F32, name="tr", tag="acc")
             for t in range(4):
-                c0 = G * HALF + t * P
-                nc.tensor.transpose(tr[:, t * P : (t + 1) * P], r_sb[:, c0 : c0 + P], ident[:])
+                nc.tensor.transpose(tr[:, t * P : (t + 1) * P], r_sb[:, t * P : (t + 1) * P], ident[:])
             return tr
 
         def r_keep(tr, G):
@@ -200,59 +206,47 @@ def tile_chunkdecayedstateplusundecayedwrites_kernel(tc, x, beta, k, gk, s, ga, 
 
         for g in range(GROUPS):
             for j in range(PACK):
-                rsq(g, j)
-        for G in range(2):
-            for g in range(GROUPS):
-                sqh(g, G)
-        m00 = b2_mix(0, 0)
-        m01 = b2_mix(0, 1)
-        quant(b2c, b2s, 0, 0, m00)
-        m10 = b2_mix(1, 0)
-        quant(b2c, b2s, 0, 1, m01)
-        m11 = b2_mix(1, 1)
-        quant(b2c, b2s, 1, 0, m10)
-        for g, j in B1_SCALE_ON_VECTOR:
-            b1_scale(g, j)
+                b1_scale(g, j)
         r_ps = [psum.tile([P, HALF], F32, name="r_ps%d" % G, tag="acc") for G in range(2)]
-        for G in range(2):
-            for g in range(GROUPS):
+        a1m, a2m, b1m = {}, {}, {}
+        for g in range(GROUPS):
+            for j in range(PACK):
+                rsq(g, j)
+            for G in range(2):
+                sqh(g, G)
+            if g == 0:
+                b2m = [b2_mix(i // 2, i % 2) for i in range(4)]
+                for i in range(4):
+                    quant(b2c, b2s, i // 2, i % 2, b2m[i])
+            for G in range(2):
                 for j in range(PACK):
                     delta(g, j, G)
                     r_part(r_ps[G], g, j, G)
-                if G == 0 and g == 0:
-                    quant(b2c, b2s, 1, 1, m11)
-        for g in range(GROUPS):
-            for j in range(PACK):
-                if (g, j) not in B1_SCALE_ON_VECTOR:
-                    b1_scale(g, j)
             if g == 0:
-                a1m = [a1_mix(0, 0)]
-        a2m = [a2_mix(0, 0)]
-        a2m.append(a2_mix(1, 0))
-        r_out(r_ps[0], 0)
-        a1m.append(a1_mix(1, 0))
-        r_out(r_ps[1], 1)
-        tr0 = r_turn(0)
-        tr1 = r_turn(1)
-        b1m = {}
+                a2m[0, 0] = a2_mix(0, 0)
+                a2m[0, 1] = a2_mix(0, 1)
+                quant(a2c, a2s, 0, 0, a2m[0, 0])
+                quant(a2c, a2s, 0, 1, a2m[0, 1])
+        a1m[0, 0] = a1_mix(0, 0)
+        a2m[1, 0] = a2_mix(1, 0)
         b1m[0, 0] = b1_mix(0, 0)
-        quant(a2c, a2s, 0, 0, a2m[0])
-        quant(a1c, a1s, 0, 0, a1m[0])
-        b1m[1, 0] = b1_mix(1, 0)
-        quant(a2c, a2s, 1, 0, a2m[1])
-        quant(a1c, a1s, 1, 0, a1m[1])
-        r_keep(tr0, 0)
-        r_keep(tr1, 1)
-        b1m[0, 1] = b1_mix(0, 1)
+        quant(a1c, a1s, 0, 0, a1m[0, 0])
+        a1m[1, 0] = a1_mix(1, 0)
+        quant(a2c, a2s, 1, 0, a2m[1, 0])
         quant(b1c, b1s, 0, 0, b1m[0, 0])
-        a2n = [a2_mix(0, 1)]
+        b1m[1, 0] = b1_mix(1, 0)
+        quant(a1c, a1s, 1, 0, a1m[1, 0])
+        a2m[1, 1] = a2_mix(1, 1)
         quant(b1c, b1s, 1, 0, b1m[1, 0])
-        b1m[1, 1] = b1_mix(1, 1)
+        r_sb0 = r_out(r_ps[0])
+        r_sb1 = r_out(r_ps[1])
+        tr0 = r_turn(r_sb0)
+        b1m[0, 1] = b1_mix(0, 1)
+        r_keep(tr0, 0)
+        quant(a2c, a2s, 1, 1, a2m[1, 1])
+        b1m[1, 1] = b1_mix(1, 1, nc.vector.tensor_copy)
         quant(b1c, b1s, 0, 1, b1m[0, 1])
-        a2n.append(a2_mix(1, 1))
         quant(b1c, b1s, 1, 1, b1m[1, 1])
-        quant(a2c, a2s, 0, 1, a2n[0])
-        quant(a2c, a2s, 1, 1, a2n[1])
 
         accs, sums, scale_planes = {}, {}, {}
 
@@ -277,9 +271,10 @@ def tile_chunkdecayedstateplusundecayedwrites_kernel(tc, x, beta, k, gk, s, ga, 
 
         def times_state(u):
             G, h = u
-            for t in (0, 2):
-                v = sums[u][:, t : t + 2, :]
-                nc.vector.tensor_tensor(out=v, in0=v, in1=st[G][:, t : t + 2, h * HALF : (h + 1) * HALF], op=ALU.mult)
+            step = 2 if u == units[0] else 4
+            for t in range(0, 4, step):
+                v = sums[u][:, t : t + step, :]
+                nc.vector.tensor_tensor(out=v, in0=v, in1=st[G][:, t : t + step, h * HALF : (h + 1) * HALF], op=ALU.mult)
 
         def add_write(u, lo=0, hi=HALF):
             for t in range(4):
@@ -325,26 +320,28 @@ def tile_chunkdecayedstateplusundecayedwrites_kernel(tc, x, beta, k, gk, s, ga, 
 
         products(0, "w")
         products(0, "p")
+        tr1 = r_turn(r_sb1)
         decay(units[0])
-        a1n = [a1_mix(0, 1)]
+        a1m[0, 1] = a1_mix(0, 1)
+        r_keep(tr1, 1)
         products(1, "p")
         times_state(units[0])
         decay(units[1])
-        a1n.append(a1_mix(1, 1))
+        a1m[1, 1] = a1_mix(1, 1)
         finish(0)
         products(1, "w")
         rounded[0] = round_out(units[0], mix())
+        quant(a1c, a1s, 0, 1, a1m[0, 1])
         times_state(units[1])
+        quant(a1c, a1s, 1, 1, a1m[1, 1])
         finish(1)
-        quant(a1c, a1s, 0, 1, a1n[0])
-        quant(a1c, a1s, 1, 1, a1n[1])
-        products(2, "w")
         products(2, "p")
+        products(2, "w")
+        decay(units[2])
         rounded[1] = round_out(units[1], mix())
         plane_out(units[0], rounded[0])
-        decay(units[2])
-        plane_out(units[1], rounded[1])
         times_state(units[2])
+        plane_out(units[1], rounded[1])
         products(3, "p")
         decay(units[3])
         finish(2)

@@ -21,6 +21,12 @@ PACK = 4
 GROUPS = 2
 HALF = 512
 KK_ON_GPSIMD = ((0, 3), (1, 3))
+STATE_SPLIT = {
+    (0, 0): (("v", 0, 1), ("v", 1, 3), ("g", 3, 4)),
+    (0, 1): (("g", 2, 3), ("g", 3, 4), ("v", 0, 2)),
+    (1, 0): (("g", 2, 3), ("g", 3, 4), ("v", 0, 2)),
+    (1, 1): (("g", 2, 3), ("g", 3, 4), ("v", 0, 2)),
+}
 
 
 def tile_chunkdecayedstateplusundecayedwrites_kernel(tc, x, beta, k, gk, s, ga, gb, out_0, out_1, out_2):
@@ -160,9 +166,9 @@ def tile_chunkdecayedstateplusundecayedwrites_kernel(tc, x, beta, k, gk, s, ga, 
                 in1=bt[g][:, j, G * HALF : (G + 1) * HALF].rearrange("p (m t) -> p t m", t=4),
                 op0=ALU.mult, op1=ALU.mult)
 
-        def a1_mix(g, G):
+        def a1_mix(g, G, engine_copy=nc.scalar.copy):
             m = mix()
-            nc.scalar.copy(out=outer(m[:]), in_=inner(dl[g][:, :, G * HALF : (G + 1) * HALF]))
+            engine_copy(out=outer(m[:]), in_=inner(dl[g][:, :, G * HALF : (G + 1) * HALF]))
             return m
 
         def a2_mix(g, G):
@@ -253,7 +259,7 @@ def tile_chunkdecayedstateplusundecayedwrites_kernel(tc, x, beta, k, gk, s, ga, 
         def product(u, ac, asc, bc, bsc, which):
             G, h = u
             hs = slice(h * HALF, (h + 1) * HALF)
-            for t in range(4):
+            for t in (2, 3, 0, 1) if which == "p" and u != units[0] else (0, 1, 2, 3):
                 ds = slice(G * HALF + t * P, G * HALF + (t + 1) * P)
                 acc = psum.tile([P, HALF], F32, name="acc_" + which, tag="acc")
                 for g in range(GROUPS):
@@ -266,15 +272,15 @@ def tile_chunkdecayedstateplusundecayedwrites_kernel(tc, x, beta, k, gk, s, ga, 
         def decay(u):
             G, h = u
             sums[u] = rows.tile([P, PACK, HALF], F32, name="e%d%d" % u, tag="row")
-            for t in range(4):
+            for t in (0, 1, 2, 3) if u == units[0] else (2, 3, 0, 1):
                 nc.scalar.activation(out=sums[u][:, t, :], in_=accs[u, "p", t][:], func=ACT.Exp, scale=-1.0 / N, bias=nr[:, 4 * G + t : 4 * G + t + 1])
 
         def times_state(u):
             G, h = u
-            step = 2 if u == units[0] else 4
-            for t in range(0, 4, step):
-                v = sums[u][:, t : t + step, :]
-                nc.vector.tensor_tensor(out=v, in0=v, in1=st[G][:, t : t + step, h * HALF : (h + 1) * HALF], op=ALU.mult)
+            for eng, t0, t1 in STATE_SPLIT[u]:
+                engine = nc.vector if eng == "v" else nc.gpsimd
+                v = sums[u][:, t0:t1, :]
+                engine.tensor_tensor(out=v, in0=v, in1=st[G][:, t0:t1, h * HALF : (h + 1) * HALF], op=ALU.mult)
 
         def add_write(u, lo=0, hi=HALF):
             for t in range(4):
@@ -322,29 +328,29 @@ def tile_chunkdecayedstateplusundecayedwrites_kernel(tc, x, beta, k, gk, s, ga, 
         products(0, "p")
         tr1 = r_turn(r_sb1)
         decay(units[0])
-        a1m[0, 1] = a1_mix(0, 1)
-        r_keep(tr1, 1)
         products(1, "p")
+        r_keep(tr1, 1)
+        a1m[1, 1] = a1_mix(1, 1, nc.vector.tensor_copy)
+        a1m[0, 1] = a1_mix(0, 1)
         times_state(units[0])
         decay(units[1])
-        a1m[1, 1] = a1_mix(1, 1)
         finish(0)
         products(1, "w")
-        rounded[0] = round_out(units[0], mix())
-        quant(a1c, a1s, 0, 1, a1m[0, 1])
-        times_state(units[1])
         quant(a1c, a1s, 1, 1, a1m[1, 1])
-        finish(1)
+        quant(a1c, a1s, 0, 1, a1m[0, 1])
+        rounded[0] = round_out(units[0], mix())
         products(2, "p")
-        products(2, "w")
+        times_state(units[1])
         decay(units[2])
-        rounded[1] = round_out(units[1], mix())
+        finish(1)
+        products(2, "w")
         plane_out(units[0], rounded[0])
+        rounded[1] = round_out(units[1], mix())
         times_state(units[2])
-        plane_out(units[1], rounded[1])
         products(3, "p")
         decay(units[3])
         finish(2)
+        plane_out(units[1], rounded[1])
         products(3, "w")
         rounded[2] = round_out(units[2], mix())
         times_state(units[3])

from contextlib import ExitStack

import concourse.mybir as mybir
from concourse.masks import make_identity

T, D, N = 1024, 1024, 1024
FLOPS = 2 * 2 * T * D * N + 2 * T * D

F32 = mybir.dt.float32
BF16 = mybir.dt.bfloat16
U32 = mybir.dt.uint32
I32 = mybir.dt.int32
U8 = mybir.dt.uint8
FP8X4 = mybir.dt.float8_e4m3fn_x4
ACT = mybir.ActivationFunctionType
ALU = mybir.AluOpType
AX = mybir.AxisListType

P = 128
PACK = 4
GROUPS = 2
HALF = 512
KK_ON_GPSIMD = ((0, 3), (1, 3))
STATE_SPLIT = {
    (0, 0): (("v", 0, 1), ("v", 1, 3), ("g", 3, 4)),
    (0, 1): (("g", 2, 3), ("g", 3, 4), ("v", 0, 2)),
    (1, 0): (("g", 2, 3), ("g", 3, 4), ("v", 0, 2)),
    (1, 1): (("g", 2, 3), ("g", 3, 4), ("v", 0, 2)),
}


def tile_chunkdecayedstateplusundecayedwrites_kernel(tc, x, beta, k, gk, s, ga, gb, out_0, out_1, out_2):
    nc = tc.nc
    with ExitStack() as ctx:
        const = ctx.enter_context(tc.tile_pool(name="const", bufs=1))
        rows = ctx.enter_context(tc.tile_pool(name="rows", bufs=8))
        big = ctx.enter_context(tc.tile_pool(name="big", bufs=6))
        mixed = ctx.enter_context(tc.tile_pool(name="mixed", bufs=6))
        codes = ctx.enter_context(tc.tile_pool(name="codes", bufs=1))
        planes = ctx.enter_context(tc.tile_pool(name="planes", bufs=2))
        psum = ctx.enter_context(tc.psum_pool(name="psum", bufs=8))
        ctx.enter_context(tc.manual_schedule())

        gk_row = const.tile([P, N], BF16, name="gk_row")
        ones = const.tile([P, P], BF16, name="ones")
        warm = const.tile([P, 1], F32, name="warm")
        gab = const.tile([P, 8], BF16, name="gab")
        gbb = const.tile([P, 8], BF16, name="gbb")
        gb_up = const.tile([P, 8], F32, name="gb_up")
        gb_r = const.tile([P, 8], F32, name="gb_r")
        msq = const.tile([P, 8], F32, name="msq")
        nr = const.tile([P, 8], F32, name="nr")

        ident = const.tile([P, P], F32, name="ident")
        nc.vector.memset(gk_row[:], 0.0)
        nc.vector.memset(ones[:], 1.0)
        make_identity(nc, ident[:])
        ident_b = const.tile([P, P], BF16, name="ident_b")
        nc.gpsimd.tensor_copy(out=ident_b[:], in_=ident[:])
        gk_sb = const.tile([P, N], BF16, name="gk_sb")
        nc.scalar.dma_start(out=gbb[:].rearrange("p (g j) -> p g j", g=2), in_=gb.rearrange("(g p j) -> p g j", g=2, j=PACK))
        nc.scalar.dma_start(out=gab[:].rearrange("p (g j) -> p g j", g=2), in_=ga.rearrange("(g p j) -> p g j", g=2, j=PACK))
        nc.scalar.activation(out=warm[:], in_=ones[:, 0:1], func=ACT.Abs_reciprocal_sqrt)

        def load(name, src, g):
            t = rows.tile([P, PACK, 1024], BF16, name=name, tag="row")
            return t, src[g * 512 : (g + 1) * 512, :].rearrange("(p j) c -> p j c", j=PACK)

        kt, bt, xt, st = [], [], [], []
        for g in range(GROUPS):
            t, view = load("k%d" % g, k, g)
            step = 1 if g == 0 else 2
            for j in range(0, PACK, step):
                nc.sync.dma_start(out=t[:, j : j + step, :], in_=view[:, j : j + step, :])
                if g == 0 and j == 0:
                    nc.sync.dma_start(out=gk_row[0:1, :], in_=gk.rearrange("(o n) -> o n", o=1))
            kt.append(t)
        for lst, src, name in ((bt, beta, "b"), (xt, x, "x"), (st, s, "s")):
            for g in range(GROUPS):
                t, view = load("%s%d" % (name, g), src, g)
                nc.sync.dma_start(out=t[:], in_=view)
                lst.append(t)

        gk_ps = []
        for h in range(2):
            ps = psum.tile([P, HALF], F32, name="gk_ps%d" % h, tag="acc")
            nc.tensor.matmul(out=ps[:], lhsT=ones[:], rhs=gk_row[:, h * HALF : (h + 1) * HALF], start=True, stop=True)
            gk_ps.append(ps)
            nc.scalar.copy(out=gk_sb[:, h * HALF : (h + 1) * HALF], in_=ps[:])
        gb_ps = psum.tile([P, HALF], F32, name="gb_ps", tag="acc")
        nc.tensor.matmul(out=gb_ps[:, 0:8], lhsT=ident_b[:], rhs=gbb[:], start=True, stop=True)

        kk = [big.tile([P, PACK, N], F32, name="kk%d" % g, tag="big") for g in range(GROUPS)]
        kk2 = [big.tile([P, PACK, N], F32, name="kks%d" % g, tag="big") for g in range(GROUPS)]
        dl = [big.tile([P, PACK, D], F32, name="dl%d" % g, tag="big") for g in range(GROUPS)]
        def scale_keys(g, j0, j1):
            for h in range(2):
                hs = slice(h * HALF, (h + 1) * HALF)
                nc.vector.tensor_tensor(
                    out=kk[g][:, j0:j1, hs], in0=kt[g][:, j0:j1, hs],
                    in1=gk_ps[h][:].unsqueeze(1).to_broadcast([P, j1 - j0, HALF]), op=ALU.mult)

        def square(g, j):
            c = 4 * g + j
            nc.scalar.activation(out=kk2[g][:, j, :], in_=kk[g][:, j, :], func=ACT.Square, scale=1.0 / 32.0, accum_out=msq[:, c : c + 1])

        nc.gpsimd.tensor_scalar(out=gb_up[:], in0=gbb[:], scalar1=1024.0, scalar2=0.0, op0=ALU.mult, op1=ALU.add)
        nc.gpsimd.tensor_scalar(out=gb_r[:], in0=gbb[:], scalar1=-1.0 / 1024.0, scalar2=0.0, op0=ALU.mult, op1=ALU.add)
        for g, j in KK_ON_GPSIMD:
            nc.gpsimd.tensor_tensor(out=kk[g][:, j, :], in0=kt[g][:, j, :], in1=gk_sb[:], op=ALU.mult)
        for j in range(3):
            scale_keys(0, j, j + 1)
            square(0, j)
        square(0, 3)
        scale_keys(1, 0, 2)
        scale_keys(1, 2, 3)
        for j in range(PACK):
            square(1, j)

        def operand(name):
            c = [codes.tile([P, 1024], U32, name="%s_c%d" % (name, g), align_bytes=64) for g in range(GROUPS)]
            z = [codes.tile([P, 1024], U8, name="%s_s%d" % (name, g), align_bytes=64) for g in range(GROUPS)]
            return c, z

        b1c, b1s = operand("b1")
        b2c, b2s = operand("b2")
        a1c, a1s = operand("a1")
        a2c, a2s = operand("a2")

        def mix():
            return mixed.tile([P, HALF, PACK], BF16, name="mix", tag="mix", align_bytes=64)

        def quant(op_c, op_s, g, h, m):
            hs = slice(h * HALF, (h + 1) * HALF)
            nc.vector.quantize_mx(out=op_c[g][:, hs].bitcast(FP8X4), scales=op_s[g][:, hs], in_=m[:].rearrange("p c j -> p (c j)"))

        def outer(m):
            return m.rearrange("p (c i) j -> p c j i", i=4)

        def inner(t):
            return t.rearrange("p j (c i) -> p c j i", i=4)

        def b2_mix(g, h):
            m = mix()
            hs = slice(h * HALF, (h + 1) * HALF)
            gbv = gb_ps[:, 4 * g : 4 * g + 4].unsqueeze(1).unsqueeze(3).to_broadcast([P, HALF // 4, PACK, 4])
            nc.vector.tensor_tensor(out=outer(m[:]), in0=inner(kk[g][:, :, hs]), in1=gbv, op=ALU.mult)
            return m

        def rsq(g, j):
            c = 4 * g + j
            nc.scalar.activation(
                out=dl[g][:, j, :].rearrange("p (G t m) -> p G t m", G=2, t=4),
                in_=bt[g][:, j, :].rearrange("p (G m t) -> p G t m", G=2, t=4),
                func=ACT.Abs_reciprocal_sqrt, scale=msq[:, c : c + 1], bias=1.0)

        def sqh(g, G):
            v = dl[g][:, :, G * HALF : (G + 1) * HALF]
            nc.scalar.activation(out=v, in_=v, func=ACT.Square)

        def delta(g, j, G):
            c = 4 * g + j
            v = dl[g][:, j, G * HALF : (G + 1) * HALF].rearrange("p (t m) -> p t m", t=4)
            nc.vector.scalar_tensor_tensor(
                out=v, in0=v, scalar=gab[:, c : c + 1],
                in1=bt[g][:, j, G * HALF : (G + 1) * HALF].rearrange("p (m t) -> p t m", t=4),
                op0=ALU.mult, op1=ALU.mult)

        def a1_mix(g, G, engine_copy=nc.scalar.copy):
            m = mix()
            engine_copy(out=outer(m[:]), in_=inner(dl[g][:, :, G * HALF : (G + 1) * HALF]))
            return m

        def a2_mix(g, G):
            m = mix()
            xv = xt[g][:, :, G * HALF : (G + 1) * HALF].rearrange("p j (m t) -> p t j m", t=4)
            for t in range(4):
                c0 = G * HALF + t * P
                nc.vector.tensor_tensor(
                    out=outer(m[:, t * P : (t + 1) * P, :]), in0=inner(dl[g][:, :, c0 : c0 + P]),
                    in1=inner(xv[:, t]), op=ALU.mult)
            return m

        def b1_scale(g, j):
            c = 4 * g + j
            v = kk2[g][:, j, :]
            nc.gpsimd.tensor_scalar(out=v, in0=v, scalar1=-1.0 / 1024.0, scalar2=gb_up[:, c : c + 1], op0=ALU.add, op1=ALU.mult)

        def b1_mix(g, h, engine_copy=nc.scalar.copy):
            m = mix()
            src = inner(kk2[g][:, :, h * HALF : (h + 1) * HALF])
            engine_copy(out=outer(m[:]), in_=src)
            return m

        def r_part(r_ps, g, j, G):
            c = 4 * g + j
            nc.tensor.matmul(out=r_ps[:], lhsT=gb_r[:, c : c + 1].to_broadcast([P, P]), rhs=dl[g][:, j, G * HALF : (G + 1) * HALF], start=(c == 0), stop=(c == 7))

        def r_out(r_ps):
            r_sb = planes.tile([P, HALF], F32, name="r_sb", tag="w", align_bytes=64)
            nc.scalar.copy(out=r_sb[:], in_=r_ps[:])
            return r_sb

        def r_turn(r_sb):
            tr = psum.tile([P, HALF], F32, name="tr", tag="acc")
            for t in range(4):
                nc.tensor.transpose(tr[:, t * P : (t + 1) * P], r_sb[:, t * P : (t + 1) * P], ident[:])
            return tr

        def r_keep(tr, G):
            nc.vector.tensor_copy(out=nr[:, 4 * G : 4 * G + 4], in_=tr[:].rearrange("p (t m) -> p t m", t=4)[:, :, 0])

        for g in range(GROUPS):
            for j in range(PACK):
                b1_scale(g, j)
        r_ps = [psum.tile([P, HALF], F32, name="r_ps%d" % G, tag="acc") for G in range(2)]
        a1m, a2m, b1m = {}, {}, {}
        for g in range(GROUPS):
            for j in range(PACK):
                rsq(g, j)
            for G in range(2):
                sqh(g, G)
            if g == 0:
                b2m = [b2_mix(i // 2, i % 2) for i in range(4)]
                for i in range(4):
                    quant(b2c, b2s, i // 2, i % 2, b2m[i])
            for G in range(2):
                for j in range(PACK):
                    delta(g, j, G)
                    r_part(r_ps[G], g, j, G)
            if g == 0:
                a2m[0, 0] = a2_mix(0, 0)
                a2m[0, 1] = a2_mix(0, 1)
                quant(a2c, a2s, 0, 0, a2m[0, 0])
                quant(a2c, a2s, 0, 1, a2m[0, 1])
        a1m[0, 0] = a1_mix(0, 0)
        a2m[1, 0] = a2_mix(1, 0)
        b1m[0, 0] = b1_mix(0, 0)
        quant(a1c, a1s, 0, 0, a1m[0, 0])
        a1m[1, 0] = a1_mix(1, 0)
        quant(a2c, a2s, 1, 0, a2m[1, 0])
        quant(b1c, b1s, 0, 0, b1m[0, 0])
        b1m[1, 0] = b1_mix(1, 0)
        quant(a1c, a1s, 1, 0, a1m[1, 0])
        a2m[1, 1] = a2_mix(1, 1)
        quant(b1c, b1s, 1, 0, b1m[1, 0])
        r_sb0 = r_out(r_ps[0])
        r_sb1 = r_out(r_ps[1])
        tr0 = r_turn(r_sb0)
        b1m[0, 1] = b1_mix(0, 1)
        r_keep(tr0, 0)
        quant(a2c, a2s, 1, 1, a2m[1, 1])
        b1m[1, 1] = b1_mix(1, 1, nc.vector.tensor_copy)
        quant(b1c, b1s, 0, 1, b1m[0, 1])
        quant(b1c, b1s, 1, 1, b1m[1, 1])

        accs, sums, scale_planes = {}, {}, {}

        def product(u, ac, asc, bc, bsc, which):
            G, h = u
            hs = slice(h * HALF, (h + 1) * HALF)
            for t in (2, 3, 0, 1) if which == "p" and u != units[0] else (0, 1, 2, 3):
                ds = slice(G * HALF + t * P, G * HALF + (t + 1) * P)
                acc = psum.tile([P, HALF], F32, name="acc_" + which, tag="acc")
                for g in range(GROUPS):
                    nc.tensor.matmul_mx(
                        out=acc[:], lhsT=ac[g][:, ds].bitcast(FP8X4), lhsT_scale=asc[g][:, ds],
                        rhs=bc[g][:, hs].bitcast(FP8X4), rhs_scale=bsc[g][:, hs],
                        start=(g == 0), stop=(g == GROUPS - 1))
                accs[u, which, t] = acc

        def decay(u):
            G, h = u
            sums[u] = rows.tile([P, PACK, HALF], F32, name="e%d%d" % u, tag="row")
            for t in (0, 1, 2, 3) if u == units[0] else (2, 3, 0, 1):
                nc.scalar.activation(out=sums[u][:, t, :], in_=accs[u, "p", t][:], func=ACT.Exp, scale=-1.0 / N, bias=nr[:, 4 * G + t : 4 * G + t + 1])

        def times_state(u):
            G, h = u
            for eng, t0, t1 in STATE_SPLIT[u]:
                engine = nc.vector if eng == "v" else nc.gpsimd
                v = sums[u][:, t0:t1, :]
                engine.tensor_tensor(out=v, in0=v, in1=st[G][:, t0:t1, h * HALF : (h + 1) * HALF], op=ALU.mult)

        def add_write(u, lo=0, hi=HALF):
            for t in range(4):
                v = sums[u][:, t, lo:hi]
                nc.vector.scalar_tensor_tensor(out=v, in0=accs[u, "w", t][:, lo:hi], scalar=1.0 / 32.0, in1=v, op0=ALU.mult, op1=ALU.add)

        def store(u, lo=0, hi=HALF):
            G, h = u
            nc.sync.dma_start(
                out=out_0[G * 512 : (G + 1) * 512, h * HALF + lo : h * HALF + hi].rearrange("(p t) n -> p t n", t=4), in_=sums[u][:, :, lo:hi])

        def round_out(u, m, lo=0, hi=HALF, engine_copy=nc.scalar.copy):
            engine_copy(out=outer(m[:, lo:hi, :]), in_=inner(sums[u][:, :, lo:hi]))
            return m

        words = {}

        def plane_out(u, m, lo=0, hi=HALF):
            G, h = u
            if lo == 0:
                words[u] = planes.tile([P, HALF], U32, name="w_out", tag="w", align_bytes=64)
            if h == 0:
                scale_planes[G] = planes.tile([P, N], U8, name="s_out", tag="s", align_bytes=64)
            w, z = words[u], scale_planes[G]
            cols = slice(h * HALF + lo, h * HALF + hi)
            nc.vector.quantize_mx(out=w[:, lo:hi].bitcast(FP8X4), scales=z[:, cols], in_=m[:, lo:hi, :].rearrange("p c j -> p (c j)"))
            nc.sync.dma_start(out=out_1[G][:, cols, :].rearrange("p n j -> p (n j)").bitcast(I32), in_=w[:, lo:hi].bitcast(I32))
            if h == 1 and hi == HALF:
                queue = nc.sync if G == 0 else nc.scalar
                for q in range(4):
                    queue.dma_start(out=out_2[G][4 * q : 4 * q + 4, :].bitcast(I32), in_=z[32 * q : 32 * q + 4, :].bitcast(I32))

        units = [(0, 0), (0, 1), (1, 0), (1, 1)]
        A1, B1, A2, B2 = (a1c, a1s), (b1c, b1s), (a2c, a2s), (b2c, b2s)
        rounded = {}

        def finish(i):
            add_write(units[i])
            store(units[i])

        def products(i, which):
            product(units[i], *((A1 + B1) if which == "p" else (A2 + B2)), which)

        products(0, "w")
        products(0, "p")
        tr1 = r_turn(r_sb1)
        decay(units[0])
        products(1, "p")
        r_keep(tr1, 1)
        a1m[1, 1] = a1_mix(1, 1, nc.vector.tensor_copy)
        a1m[0, 1] = a1_mix(0, 1)
        times_state(units[0])
        decay(units[1])
        finish(0)
        products(1, "w")
        quant(a1c, a1s, 1, 1, a1m[1, 1])
        quant(a1c, a1s, 0, 1, a1m[0, 1])
        rounded[0] = round_out(units[0], mix())
        products(2, "p")
        times_state(units[1])
        decay(units[2])
        finish(1)
        products(2, "w")
        plane_out(units[0], rounded[0])
        rounded[1] = round_out(units[1], mix())
        times_state(units[2])
        products(3, "p")
        decay(units[3])
        finish(2)
        plane_out(units[1], rounded[1])
        products(3, "w")
        rounded[2] = round_out(units[2], mix())
        times_state(units[3])
        plane_out(units[2], rounded[2])
        last, m = units[3], mix()
        for lo in (0, 256):
            add_write(last, lo, lo + 256)
            store(last, lo, lo + 256)
        for lo, engine_copy in ((0, nc.scalar.copy), (256, nc.vector.tensor_copy)):
            round_out(last, m, lo, lo + 256, engine_copy)
        for lo in (0, 256):
            plane_out(last, m, lo, lo + 256)
